import numpy as np
import ml_dtypes


def mxq(x, axis, fmt="e4m3"):
    dtype, down = {"e4m3": (ml_dtypes.float8_e4m3fn, 7), "e5m2": (ml_dtypes.float8_e5m2, 14)}[fmt]
    v = np.moveaxis(np.asarray(x, np.float32).astype(ml_dtypes.bfloat16).astype(np.float64), axis, -1)
    blocks = v.reshape(v.shape[:-1] + (-1, 32))
    amax = np.abs(blocks).max(-1, keepdims=True)
    byte = np.maximum(np.where(amax > 0, np.frexp(amax)[1] - 1 + 127, 0) - down, 1)
    scale = np.exp2(byte - 127.0)
    codes = (blocks / scale).astype(np.float32).astype(dtype).astype(np.float64)
    return np.moveaxis((codes * scale).reshape(v.shape), -1, axis)


WIDE = False


def mx_kscale(k):
    if not WIDE:
        return np.ones(k)
    levels = np.array([10, -10, 5, -5, 0])
    if k % 512:
        return np.exp2(np.random.permutation(np.resize(levels, k // 32))).repeat(32)
    a = np.empty((k // 512, 16))
    for p in range(k // 512):
        a[p, :8] = np.random.permutation(np.resize(levels, 8))
        for g in range(8):
            far = levels[np.abs(levels - a[p, g]) >= 10]
            a[p, g + 8] = far[np.random.randint(len(far))]
    return np.exp2(a.ravel()).repeat(32)


def f64(x):
    return np.asarray(x).astype(np.float64)


def striped(idx):
    return np.tile(idx.reshape(-1, 16).T, (8, 1)).astype(np.uint16)


def unstriped(offs):
    return offs[:16].T.reshape(-1).astype(np.int64)


E2M1 = np.array([0.0, 0.5, 1.0, 1.5, 2.0, 3.0, 4.0, 6.0, -0.0, -0.5, -1.0, -1.5, -2.0, -3.0, -4.0, -6.0])


def pack_weight(w, fmt):
    k, n = w.shape
    w = f64(np.asarray(w, np.float32).astype(ml_dtypes.bfloat16)).reshape(k // 32, 32, n)
    amax = np.abs(w).max(1)
    if fmt == "e4m3":
        byte = np.frexp(amax)[1] - 1 + 127 - 7
    else:
        mant, ex = np.frexp(amax / 6.0)
        byte = np.where(mant > 0.5, ex, ex - 1) + 127
    byte = np.clip(np.where(amax > 0, byte, 1), 1, 254)
    scaled = (w * np.exp2(127.0 - byte)[:, None, :]).reshape(k, n).astype(np.float32)
    by_word = np.ascontiguousarray(scaled.reshape(k // 512, 128, 4, n).transpose(0, 1, 3, 2))
    if fmt == "e4m3":
        words = by_word.astype(ml_dtypes.float8_e4m3fn).view(np.uint8)
    else:
        c = by_word.astype(ml_dtypes.float4_e2m1fn).view(np.uint8) & 0xF
        words = (c[..., 0::2] | (c[..., 1::2] << 4)).reshape(k // 512, 128, 2 * n)
    return np.ascontiguousarray(words), np.ascontiguousarray(byte.astype(np.uint8).reshape(k // 512, 16, n))


def unpack_weight(words, scales, fmt):
    g, _, n = scales.shape
    words = np.ascontiguousarray(words).reshape(g, 128, n, -1)
    if fmt == "e4m3":
        vals = words.view(ml_dtypes.float8_e4m3fn).astype(np.float64)
    else:
        nib = np.empty((g, 128, n, 4), np.uint8)
        nib[..., 0::2] = words & 0xF
        nib[..., 1::2] = words >> 4
        vals = E2M1[nib]
    vals = vals * np.repeat(np.exp2(scales.astype(np.float64) - 127.0), 8, axis=1)[..., None]
    return vals.transpose(0, 1, 3, 2).reshape(g * 512, n)


def gelu(v):
    return 0.5 * v * (1.0 + np.tanh(np.sqrt(2.0 / np.pi) * (v + 0.044715 * v**3)))


def bf(x):
    return np.asarray(x, np.float32).astype(ml_dtypes.bfloat16)


def planes(Y):
    n, m = Y.shape
    b = f64(bf(Y)).reshape(n // 32, 32, m)
    amax = np.abs(b).max(1)
    byte = np.clip(np.where(amax > 0, np.frexp(amax)[1] - 1 + 127 - 7, 1), 1, 254)
    codes = (b * np.exp2(127.0 - byte)[:, None, :]).reshape(n, m).astype(np.float32).astype(ml_dtypes.float8_e4m3fn).view(np.uint8)
    words = codes.reshape(n // 512, 128, 4, m).transpose(0, 1, 3, 2)
    return np.ascontiguousarray(words), np.ascontiguousarray(byte.astype(np.uint8).reshape(n // 512, 16, m))


K, T, S, P, H, N = 512, 4096, 1024, 512, 1536, 512

def setup_inputs():
    n = np.random.standard_normal
    s = mx_kscale(K)[:, None]
    u = mx_kscale(H)[:, None]
    tab_words, tab_scales = pack_weight(n((K, T)) * s, "e4m3")
    w4_words, w4_scales = pack_weight(n((H, N)) / np.sqrt(H) / u, "e2m1")
    return {
        "tab_words": tab_words, "tab_scales": tab_scales,
        "offs": striped(np.random.permutation(T)[:S]),
        "pos1": striped(np.random.permutation(S)[:P]),
        "pos2": striped(np.random.permutation(S)[:P]),
        "w1": (0.4 * n((K, H)) / np.sqrt(K) / s).astype(np.float32),
        "phase": np.random.uniform(-0.8, 0.8, H).astype(np.float32),
        "gain": (np.random.uniform(1.5, 4.5, H) * u[:, 0]).astype(np.float32),
        "prior": (0.7 * n((H, P)) * u).astype(np.float32),
        "w4_words": w4_words, "w4_scales": w4_scales,
        "wb": (n((H, N)) / np.sqrt(H) / u * np.exp(0.8 * n(N))).astype(np.float32),
    }

def reference(tab_words, tab_scales, offs, pos1, pos2, w1, phase, gain, prior, w4_words, w4_scales, wb):
    v = unpack_weight(tab_words, tab_scales, "e4m3")[:, unstriped(offs)]
    resp = mxq(f64(w1), 0, "e4m3").T @ v
    h = resp * np.cos(resp + f64(phase)[:, None]) * f64(gain)[:, None]
    xa = h[:, unstriped(pos1)] + f64(prior)
    xb = np.abs(h[:, unstriped(pos2)])
    w4 = unpack_weight(w4_words, w4_scales, "e2m1")
    ya = w4.T @ mxq(xa, 0, "e4m3")
    yb = mxq(f64(wb), 0, "e4m3").T @ mxq(xb, 0, "e4m3")
    y = ya * yb
    words, scales = planes(y)
    return y, words, scales

@@ -1,0 +1,297 @@
+import math
+from contextlib import ExitStack
+
+import concourse.mybir as mybir
+
+K, T, S, J, H, N = 512, 4096, 1024, 512, 1536, 512
+FLOPS = 2 * K * H * S + 2 * 2 * H * N * J
+
+F32 = mybir.dt.float32
+BF16 = mybir.dt.bfloat16
+I32 = mybir.dt.int32
+U32 = mybir.dt.uint32
+U16 = mybir.dt.uint16
+U8 = mybir.dt.uint8
+FP8X4 = mybir.dt.float8_e4m3fn_x4
+FP4X4 = mybir.dt.float4_e2m1fn_x4
+ACT = mybir.ActivationFunctionType
+ALU = mybir.AluOpType
+
+P = 128
+PACK = 4
+PASS = P * PACK
+BLOCKS = H // PASS
+BANK = 512
+HALF = J // 2
+
+
+def tile_list_electrode_mapping_features_kernel(
+    tc, tab_words, tab_scales, offs, pos1, pos2, w1, phase, gain, prior, w4_words, w4_scales, wb, out_0, out_1, out_2
+):
+    nc = tc.nc
+    with ExitStack() as ctx:
+        lists = ctx.enter_context(tc.tile_pool(name="lists", bufs=1))
+        keep = ctx.enter_context(tc.tile_pool(name="keep", bufs=1))
+        ring = ctx.enter_context(tc.tile_pool(name="ring", bufs=2))
+        psum = ctx.enter_context(tc.psum_pool(name="psum", bufs=4))
+
+        offs_t = lists.tile([P, S // 16], U16, name="offs_t")
+        pos1_t = lists.tile([P, J // 16], U16, name="pos1_t")
+        pos2_t = lists.tile([P, J // 16], U16, name="pos2_t")
+        table_words = keep.tile([P, T], U32, name="table_words", align_bytes=64)
+        table_scales = keep.tile([P, T], U8, name="table_scales", align_bytes=64)
+        w4_raw = keep.tile([P, BLOCKS * N * 2], U8, name="w4_raw", align_bytes=64)
+        w4_raw_scales = keep.tile([P, BLOCKS, N], U8, name="w4_raw_scales", align_bytes=64)
+        phase_t = keep.tile([P, BLOCKS, PACK], F32, name="phase_t")
+        gain_t = keep.tile([P, BLOCKS, PACK], F32, name="gain_t")
+        w1_raw = [keep.tile([P, PACK, PASS], F32, name=f"w1_raw{b}") for b in range(BLOCKS)]
+        wb_raw = [ring.tile([P, PACK, N], F32, name="wb_raw") for b in range(BLOCKS)]
+        prior_t = [ring.tile([P, PACK, J], F32, name="prior_t") for b in range(BLOCKS)]
+
+        def load_w1(b):
+            nc.sync.dma_start(out=w1_raw[b][:], in_=w1[:, b * PASS : (b + 1) * PASS].rearrange("(p i) c -> p i c", i=PACK))
+
+        def load_rows(dst, src, b):
+            nc.sync.dma_start(out=dst[b][:], in_=src[b * PASS : (b + 1) * PASS, :].rearrange("(p i) c -> p i c", i=PACK))
+
+        nc.vector.memset(table_scales[:].bitcast(I32), 0)
+        nc.gpsimd.memset(w4_raw_scales[:].rearrange("p a n -> p (a n)").bitcast(I32), 0)
+        nc.sync.dma_start(offs_t[:], offs)
+        load_w1(0)
+        for q in range(4):
+            nc.sync.dma_start(
+                out=table_scales[32 * q : 32 * q + 4, :].bitcast(I32), in_=tab_scales[0, 4 * q : 4 * q + 4, :].bitcast(I32)
+            )
+        nc.sync.dma_start(out=table_words[:].bitcast(I32), in_=tab_words[0].rearrange("p t i -> p (t i)").bitcast(I32))
+        nc.sync.dma_start(out=phase_t[:], in_=phase.rearrange("(b p t) -> p b t", p=P, t=PACK))
+        nc.sync.dma_start(out=gain_t[:], in_=gain.rearrange("(b p t) -> p b t", p=P, t=PACK))
+        nc.sync.dma_start(pos2_t[:], pos2)
+        nc.sync.dma_start(pos1_t[:], pos1)
+        load_rows(prior_t, prior, 0)
+        nc.sync.dma_start(
+            out=w4_raw[:].bitcast(I32).rearrange("p (a c) -> p a c", a=BLOCKS),
+            in_=w4_words.bitcast(I32).rearrange("a p c -> p a c"),
+        )
+        for q in range(4):
+            nc.sync.dma_start(
+                out=w4_raw_scales[32 * q : 32 * q + 4, :, :].bitcast(I32),
+                in_=w4_scales[:, 4 * q : 4 * q + 4, :].bitcast(I32).rearrange("a r c -> r a c"),
+            )
+        load_w1(1)
+        load_rows(wb_raw, wb, 0)
+        load_rows(prior_t, prior, 1)
+        load_w1(2)
+        load_rows(wb_raw, wb, 1)
+        load_rows(prior_t, prior, 2)
+        load_rows(wb_raw, wb, 2)
+
+        def quantize(name, rounded, width):
+            codes = keep.tile([P, width], U32, name=name + "_codes", align_bytes=64)
+            scales = keep.tile([P, width], U8, name=name + "_scales", align_bytes=64)
+            nc.vector.quantize_mx(out=codes[:].bitcast(FP8X4), scales=scales[:], in_=rounded[:])
+            return codes, scales
+
+        def round_weight(raw, on_vector):
+            rounded = ring.tile([P, PACK * PASS], BF16, name="w_rounded", align_bytes=64)
+            dst = rounded[:].rearrange("p (t m i) -> p m i t", t=PACK, i=PACK)
+            src = raw[:].rearrange("p i (m t) -> p m i t", t=PACK)
+            if on_vector:
+                nc.vector.tensor_copy(out=dst, in_=src)
+            else:
+                nc.scalar.copy(out=dst, in_=src)
+            return rounded
+
+        def woven(rounded, planes):
+            return (
+                rounded[:].rearrange("p (c i t) -> p c t i", i=4, t=PACK),
+                planes[:].rearrange("p t (c i) -> p c t i", i=4),
+            )
+
+        v_scales = keep.tile([P, S], U8, name="v_scales", align_bytes=64)
+        nc.vector.tensor_copy(out=v_scales[:], in_=table_scales[:].indirect(offs_t[:]))
+        w1_q = {0: quantize("w1_0", round_weight(w1_raw[0], False), PASS)}
+        w4_codes = keep.tile([P, BLOCKS * N * 2], U8, name="w4_codes", align_bytes=64)
+        w4_planes = keep.tile([P, BLOCKS * N], U8, name="w4_planes", align_bytes=64)
+        v_words = []
+        for u in range(S // BANK):
+            words = keep.tile([P, BANK], U32, name=f"v_words{u}", align_bytes=64)
+            nc.vector.tensor_copy(out=words[:], in_=table_words[:].indirect(offs_t[:, u * BANK // 16 : (u + 1) * BANK // 16]))
+            v_words.append(words)
+
+        def deal_w4():
+            nc.vector.tensor_copy(
+                out=w4_codes[:].bitcast(U16).rearrange("p (a t m) -> p a m t", a=BLOCKS, t=PACK),
+                in_=w4_raw[:].bitcast(U16).rearrange("p (a m t) -> p a m t", a=BLOCKS, t=PACK),
+            )
+            nc.vector.tensor_copy(
+                out=w4_planes[:].rearrange("p (a t m) -> p a m t", a=BLOCKS, t=PACK),
+                in_=w4_raw_scales[:].rearrange("p a (m t) -> p a m t", t=PACK),
+            )
+
+        def features(b, t):
+            codes, scales = w1_q[b]
+            cols = slice(t * P, (t + 1) * P)
+            resp, folded, cosine = [], [], []
+            for u in range(S // BANK):
+                bank = psum.tile([P, BANK], F32, name="resp")
+                nc.tensor.matmul_mx(
+                    out=bank[:],
+                    lhsT=codes[:, cols].bitcast(FP8X4),
+                    lhsT_scale=scales[:, cols],
+                    rhs=v_words[u][:].bitcast(FP8X4),
+                    rhs_scale=v_scales[:, u * BANK : (u + 1) * BANK],
+                    start=True,
+                    stop=True,
+                )
+                resp.append(bank)
+            for u in range(S // BANK):
+                a = ring.tile([P, BANK], F32, name="folded", bufs=4)
+                nc.scalar.activation(out=a[:], in_=resp[u][:], func=ACT.Abs, bias=phase_t[:, b, t : t + 1])
+                folded.append(a)
+            for u in range(S // BANK):
+                c = ring.tile([P, BANK], F32, name="cosine", bufs=4)
+                nc.scalar.activation(out=c[:], in_=folded[u][:], func=ACT.Sin, scale=-1.0, bias=math.pi / 2)
+                cosine.append(c)
+            h = ring.tile([P, S], F32, name="h", bufs=5)
+            for u in range(S // BANK):
+                nc.vector.scalar_tensor_tensor(
+                    out=h[:, u * BANK : (u + 1) * BANK],
+                    in0=resp[u][:],
+                    scalar=gain_t[:, b, t : t + 1],
+                    in1=cosine[u][:],
+                    op0=ALU.mult,
+                    op1=ALU.mult,
+                )
+            return h
+
+        def pick_basal(planes, h, t, j0, width):
+            nc.vector.tensor_copy(out=planes[:, t, :], in_=h[:].indirect(pos2_t[:, j0 // 16 : (j0 + width) // 16]))
+
+        def pick_apical(planes, h, b, t, j0, width):
+            nc.vector.tensor_tensor(
+                out=planes[:, t, :],
+                in0=h[:].indirect(pos1_t[:, j0 // 16 : (j0 + width) // 16]),
+                in1=prior_t[b][:, t, j0 : j0 + width],
+                op=ALU.add,
+            )
+
+        def round_basal(planes, width):
+            rounded = ring.tile([P, PACK * width], BF16, name="x_rounded", align_bytes=64, bufs=3)
+            dst, src = woven(rounded, planes)
+            nc.scalar.activation(out=dst, in_=src, func=ACT.Abs)
+            return rounded
+
+        def round_apical(planes, width):
+            rounded = ring.tile([P, PACK * width], BF16, name="x_rounded", align_bytes=64, bufs=3)
+            dst, src = woven(rounded, planes)
+            nc.scalar.copy(out=dst, in_=src)
+            return rounded
+
+        def second_stage(banks, b, half, weight, x, x0):
+            for t in range(PACK):
+                lhsT, lhsT_scale = weight(b, t)
+                nc.tensor.matmul_mx(
+                    out=banks[half][t // 2][:, t % 2, :],
+                    lhsT=lhsT,
+                    lhsT_scale=lhsT_scale,
+                    rhs=x[0][:, x0 : x0 + HALF].bitcast(FP8X4),
+                    rhs_scale=x[1][:, x0 : x0 + HALF],
+                    start=(b == 0 and t % 2 == 0),
+                    stop=(b == BLOCKS - 1 and t % 2 == 1),
+                )
+
+        wb_q = {}
+
+        def wb_slice(b, t):
+            return wb_q[b][0][:, t * P : (t + 1) * P].bitcast(FP8X4), wb_q[b][1][:, t * P : (t + 1) * P]
+
+        def w4_slice(b, t):
+            c0 = b * N + t * P
+            return w4_codes[:, 2 * c0 : 2 * (c0 + P)].bitcast(FP4X4), w4_planes[:, c0 : c0 + P]
+
+        yb_banks = [[psum.tile([P, 2, HALF], F32, name="yb") for pair in range(2)] for half in range(2)]
+        xa_q = {}
+        last = BLOCKS - 1
+        slices = [(b, t) for b in range(BLOCKS) for t in range(PACK)]
+        hs = {slices[0]: features(*slices[0])}
+        planes_a, planes_b = None, None
+        done = None
+        for s, (b, t) in enumerate(slices):
+            width = J if b < last else HALF
+            if t == 0:
+                planes_a = ring.tile([P, PACK, width], F32, name="planes_a")
+                planes_b = ring.tile([P, PACK, width], F32, name="planes_b")
+            if t == 1 and b < last:
+                w1_q[b + 1] = quantize(f"w1_{b + 1}", round_weight(w1_raw[b + 1], False), PASS)
+            if t == 2:
+                wb_q[b] = quantize(f"wb_{b}", round_weight(wb_raw[b], True), N)
+            if s + 1 < len(slices):
+                hs[slices[s + 1]] = features(*slices[s + 1])
+            if t == 0 and done is not None:
+                xb_rounded = round_basal(done[1], J)
+                xa_rounded = round_apical(done[0], J)
+            pick_basal(planes_b, hs[b, t], t, 0, width)
+            pick_apical(planes_a, hs[b, t], b, t, 0, width)
+            if t == 0 and done is not None:
+                xb_q = quantize(f"xb_{b - 1}", xb_rounded, J)
+                xa_q[b - 1] = quantize(f"xa_{b - 1}", xa_rounded, J)
+                for half in range(2):
+                    second_stage(yb_banks, b - 1, half, wb_slice, xb_q, half * HALF)
+            if s == 0:
+                deal_w4()
+            if t == PACK - 1:
+                done = (planes_a, planes_b)
+
+        ya_banks = [[psum.tile([P, 2, HALF], F32, name="resp") for pair in range(2)] for half in range(2)]
+        for b in range(last):
+            for half in range(2):
+                second_stage(ya_banks, b, half, w4_slice, xa_q[b], half * HALF)
+
+        y_codes = keep.tile([P, J], U32, name="y_codes", align_bytes=64)
+        y_scales = keep.tile([P, J], U8, name="y_scales", align_bytes=64)
+        out_rows = out_0.rearrange("(p t) j -> p t j", t=PACK)
+        out_words = out_1[0].rearrange("p m t -> p (m t)").bitcast(I32)
+
+        def close_sums(half, xa_rounded, xb_rounded):
+            xb_q = quantize(f"xb_last{half}", xb_rounded, HALF)
+            second_stage(yb_banks, last, half, wb_slice, xb_q, 0)
+            xa_last = quantize(f"xa_last{half}", xa_rounded, HALF)
+            second_stage(ya_banks, last, half, w4_slice, xa_last, 0)
+
+        def product(half):
+            y = keep.tile([P, PACK, HALF], F32, name=f"y{half}")
+            for pair in range(2):
+                yb = ring.tile([P, 2, HALF], F32, name="yb_out")
+                nc.scalar.copy(out=yb[:], in_=yb_banks[half][pair][:])
+                nc.vector.tensor_tensor(out=y[:, 2 * pair : 2 * pair + 2, :], in0=ya_banks[half][pair][:], in1=yb[:], op=ALU.mult)
+            cols = slice(half * HALF, (half + 1) * HALF)
+            nc.sync.dma_start(out=out_rows[:, :, cols], in_=y[:])
+            rounded = ring.tile([P, PACK * HALF], BF16, name="w_rounded", align_bytes=64)
+            dst, src = woven(rounded, y)
+            nc.scalar.copy(out=dst, in_=src)
+            return rounded
+
+        def planes_out(half, rounded):
+            cols = slice(half * HALF, (half + 1) * HALF)
+            nc.vector.quantize_mx(out=y_codes[:, cols].bitcast(FP8X4), scales=y_scales[:, cols], in_=rounded[:])
+            nc.sync.dma_start(out=out_words[:, cols], in_=y_codes[:, cols].bitcast(I32))
+
+        xb_first = round_basal(done[1], HALF)
+        xa_first = round_apical(done[0], HALF)
+        planes_a = ring.tile([P, PACK, HALF], F32, name="planes_a")
+        planes_b = ring.tile([P, PACK, HALF], F32, name="planes_b")
+        for t in range(PACK):
+            pick_basal(planes_b, hs[last, t], t, HALF, HALF)
+        close_sums(0, xa_first, xb_first)
+        xb_second = round_basal(planes_b, HALF)
+        for t in range(PACK):
+            pick_apical(planes_a, hs[last, t], last, t, HALF, HALF)
+        xa_second = round_apical(planes_a, HALF)
+        y_first = product(0)
+        close_sums(1, xa_second, xb_second)
+        planes_out(0, y_first)
+        planes_out(1, product(1))
+        for q in range(4):
+            nc.sync.dma_start(
+                out=out_2[0, 4 * q : 4 * q + 4, :].bitcast(I32), in_=y_scales[32 * q : 32 * q + 4, :].bitcast(I32)
+            )

@@ -21,8 +21,14 @@ P = 128
 PACK = 4
 PASS = P * PACK
 BLOCKS = H // PASS
+LAST = BLOCKS - 1
 BANK = 512
+PARTS = S // BANK
 HALF = J // 2
+PER_COLUMN = 16
+QUADRANT = 32
+SCALE_ROWS = 16
+RUN = 4
 
 
 def tile_list_electrode_mapping_features_kernel(
@@ -33,11 +39,11 @@ def tile_list_electrode_mapping_features_kernel(
         lists = ctx.enter_context(tc.tile_pool(name="lists", bufs=1))
         keep = ctx.enter_context(tc.tile_pool(name="keep", bufs=1))
         ring = ctx.enter_context(tc.tile_pool(name="ring", bufs=2))
-        psum = ctx.enter_context(tc.psum_pool(name="psum", bufs=4))
+        psum = ctx.enter_context(tc.psum_pool(name="psum", bufs=8))
 
-        offs_t = lists.tile([P, S // 16], U16, name="offs_t")
-        pos1_t = lists.tile([P, J // 16], U16, name="pos1_t")
-        pos2_t = lists.tile([P, J // 16], U16, name="pos2_t")
+        offs_t = lists.tile([P, S // PER_COLUMN], U16, name="offs_t")
+        pos1_t = lists.tile([P, J // PER_COLUMN], U16, name="pos1_t")
+        pos2_t = lists.tile([P, J // PER_COLUMN], U16, name="pos2_t")
         table_words = keep.tile([P, T], U32, name="table_words", align_bytes=64)
         table_scales = keep.tile([P, T], U8, name="table_scales", align_bytes=64)
         w4_raw = keep.tile([P, BLOCKS * N * 2], U8, name="w4_raw", align_bytes=64)
@@ -54,30 +60,38 @@ def tile_list_electrode_mapping_features_kernel(
         def load_rows(dst, src, b):
             nc.sync.dma_start(out=dst[b][:], in_=src[b * PASS : (b + 1) * PASS, :].rearrange("(p i) c -> p i c", i=PACK))
 
+        def load_per_row(dst, src):
+            nc.sync.dma_start(out=dst[:], in_=src.rearrange("(b p t) -> p b t", p=P, t=PACK))
+
+        warm = keep.tile([P, 1], F32, name="warm")
+        warm_out = keep.tile([P, 1], F32, name="warm_out")
         nc.vector.memset(table_scales[:].bitcast(I32), 0)
         nc.gpsimd.memset(w4_raw_scales[:].rearrange("p a n -> p (a n)").bitcast(I32), 0)
+
         nc.sync.dma_start(offs_t[:], offs)
         load_w1(0)
-        for q in range(4):
+        for r in range(PACK):
             nc.sync.dma_start(
-                out=table_scales[32 * q : 32 * q + 4, :].bitcast(I32), in_=tab_scales[0, 4 * q : 4 * q + 4, :].bitcast(I32)
+                out=table_scales[r:P:QUADRANT, :].bitcast(I32), in_=tab_scales[0, r:SCALE_ROWS:PACK, :].bitcast(I32)
             )
+        nc.gpsimd.memset(warm[:], 0.0)
+        nc.scalar.activation(out=warm_out[:], in_=warm[:], func=ACT.Sin)
         nc.sync.dma_start(out=table_words[:].bitcast(I32), in_=tab_words[0].rearrange("p t i -> p (t i)").bitcast(I32))
-        nc.sync.dma_start(out=phase_t[:], in_=phase.rearrange("(b p t) -> p b t", p=P, t=PACK))
-        nc.sync.dma_start(out=gain_t[:], in_=gain.rearrange("(b p t) -> p b t", p=P, t=PACK))
-        nc.sync.dma_start(pos2_t[:], pos2)
-        nc.sync.dma_start(pos1_t[:], pos1)
-        load_rows(prior_t, prior, 0)
         nc.sync.dma_start(
             out=w4_raw[:].bitcast(I32).rearrange("p (a c) -> p a c", a=BLOCKS),
             in_=w4_words.bitcast(I32).rearrange("a p c -> p a c"),
         )
-        for q in range(4):
-            nc.sync.dma_start(
-                out=w4_raw_scales[32 * q : 32 * q + 4, :, :].bitcast(I32),
-                in_=w4_scales[:, 4 * q : 4 * q + 4, :].bitcast(I32).rearrange("a r c -> r a c"),
-            )
+        load_per_row(phase_t, phase)
         load_w1(1)
+        for r in range(PACK):
+            nc.sync.dma_start(
+                out=w4_raw_scales[r:P:QUADRANT, :, :].bitcast(I32),
+                in_=w4_scales[:, r:SCALE_ROWS:PACK, :].bitcast(I32).rearrange("a q c -> q a c"),
+            )
+        load_per_row(gain_t, gain)
+        nc.sync.dma_start(pos2_t[:], pos2)
+        nc.sync.dma_start(pos1_t[:], pos1)
+        load_rows(prior_t, prior, 0)
         load_rows(wb_raw, wb, 0)
         load_rows(prior_t, prior, 1)
         load_w1(2)
@@ -88,52 +102,64 @@ def tile_list_electrode_mapping_features_kernel(
         def quantize(name, rounded, width):
             codes = keep.tile([P, width], U32, name=name + "_codes", align_bytes=64)
             scales = keep.tile([P, width], U8, name=name + "_scales", align_bytes=64)
-            nc.vector.quantize_mx(out=codes[:].bitcast(FP8X4), scales=scales[:], in_=rounded[:])
+            nc.vector.quantize_mx(out=codes[:].bitcast(FP8X4), scales=scales[:], in_=rounded)
             return codes, scales
 
-        def round_weight(raw, on_vector):
-            rounded = ring.tile([P, PACK * PASS], BF16, name="w_rounded", align_bytes=64)
-            dst = rounded[:].rearrange("p (t m i) -> p m i t", t=PACK, i=PACK)
-            src = raw[:].rearrange("p i (m t) -> p m i t", t=PACK)
+        def copy_on(on_vector, dst, src):
             if on_vector:
                 nc.vector.tensor_copy(out=dst, in_=src)
             else:
                 nc.scalar.copy(out=dst, in_=src)
-            return rounded
+
+        def quantize_weight(name, raw, on_vector):
+            rounded = ring.tile([P, PACK * PASS], BF16, name="w_rounded", align_bytes=64)
+            copy_on(
+                on_vector,
+                rounded[:].rearrange("p (t m i) -> p m i t", t=PACK, i=PACK),
+                raw[:].rearrange("p i (m t) -> p m i t", t=PACK),
+            )
+            return quantize(name, rounded[:], PASS)
 
         def woven(rounded, planes):
             return (
-                rounded[:].rearrange("p (c i t) -> p c t i", i=4, t=PACK),
-                planes[:].rearrange("p t (c i) -> p c t i", i=4),
+                rounded.rearrange("p (c i t) -> p c t i", i=RUN, t=PACK),
+                planes.rearrange("p t (c i) -> p c t i", i=RUN),
             )
 
         v_scales = keep.tile([P, S], U8, name="v_scales", align_bytes=64)
         nc.vector.tensor_copy(out=v_scales[:], in_=table_scales[:].indirect(offs_t[:]))
-        w1_q = {0: quantize("w1_0", round_weight(w1_raw[0], False), PASS)}
+        w1_q = {0: quantize_weight("w1_0", w1_raw[0], True)}
         w4_codes = keep.tile([P, BLOCKS * N * 2], U8, name="w4_codes", align_bytes=64)
-        w4_planes = keep.tile([P, BLOCKS * N], U8, name="w4_planes", align_bytes=64)
+        w4_dealt_scales = keep.tile([P, BLOCKS * N], U8, name="w4_dealt_scales", align_bytes=64)
         v_words = []
-        for u in range(S // BANK):
+        for u in range(PARTS):
             words = keep.tile([P, BANK], U32, name=f"v_words{u}", align_bytes=64)
-            nc.vector.tensor_copy(out=words[:], in_=table_words[:].indirect(offs_t[:, u * BANK // 16 : (u + 1) * BANK // 16]))
+            entries = offs_t[:, u * BANK // PER_COLUMN : (u + 1) * BANK // PER_COLUMN]
+            nc.vector.tensor_copy(out=words[:], in_=table_words[:].indirect(entries))
             v_words.append(words)
 
-        def deal_w4():
-            nc.vector.tensor_copy(
-                out=w4_codes[:].bitcast(U16).rearrange("p (a t m) -> p a m t", a=BLOCKS, t=PACK),
-                in_=w4_raw[:].bitcast(U16).rearrange("p (a m t) -> p a m t", a=BLOCKS, t=PACK),
-            )
-            nc.vector.tensor_copy(
-                out=w4_planes[:].rearrange("p (a t m) -> p a m t", a=BLOCKS, t=PACK),
-                in_=w4_raw_scales[:].rearrange("p a (m t) -> p a m t", t=PACK),
-            )
+        nc.vector.tensor_copy(
+            out=w4_codes[:].bitcast(U16).rearrange("p (a t m) -> p a t m", a=BLOCKS, t=PACK),
+            in_=w4_raw[:].bitcast(U16).rearrange("p (a m t) -> p a t m", a=BLOCKS, t=PACK),
+        )
+        nc.vector.tensor_copy(
+            out=w4_dealt_scales[:].rearrange("p (a t m) -> p a t m", a=BLOCKS, t=PACK),
+            in_=w4_raw_scales[:].rearrange("p a (m t) -> p a t m", t=PACK),
+        )
 
-        def features(b, t):
+        def like(flat, other):
+            return flat if len(other.shape) == 2 else flat.rearrange("p (r j) -> p r j", r=other.shape[1])
+
+        def scratch(name):
+            return ring.tile([P, BANK], F32, name=name, bufs=2 * PARTS)[:]
+
+        def features(b, t, cosine):
+            folded = [scratch("folded") for u in range(PARTS)]
             codes, scales = w1_q[b]
             cols = slice(t * P, (t + 1) * P)
-            resp, folded, cosine = [], [], []
-            for u in range(S // BANK):
-                bank = psum.tile([P, BANK], F32, name="resp")
+            resp = []
+            for u in range(PARTS):
+                bank = psum.tile([P, BANK], F32, name="bank")
                 nc.tensor.matmul_mx(
                     out=bank[:],
                     lhsT=codes[:, cols].bitcast(FP8X4),
@@ -144,154 +170,180 @@ def tile_list_electrode_mapping_features_kernel(
                     stop=True,
                 )
                 resp.append(bank)
-            for u in range(S // BANK):
-                a = ring.tile([P, BANK], F32, name="folded", bufs=4)
-                nc.scalar.activation(out=a[:], in_=resp[u][:], func=ACT.Abs, bias=phase_t[:, b, t : t + 1])
-                folded.append(a)
-            for u in range(S // BANK):
-                c = ring.tile([P, BANK], F32, name="cosine", bufs=4)
-                nc.scalar.activation(out=c[:], in_=folded[u][:], func=ACT.Sin, scale=-1.0, bias=math.pi / 2)
-                cosine.append(c)
-            h = ring.tile([P, S], F32, name="h", bufs=5)
-            for u in range(S // BANK):
+            for u in range(PARTS):
+                nc.scalar.activation(out=folded[u], in_=resp[u][:], func=ACT.Abs, bias=phase_t[:, b, t : t + 1])
+            for u in range(PARTS):
+                nc.scalar.activation(out=cosine[u], in_=like(folded[u], cosine[u]), func=ACT.Sin, scale=-1.0, bias=math.pi / 2)
+            if b < LAST:
+                h = ring.tile([P, S], F32, name="h", bufs=3)
+            else:
+                h = ring.tile([P, S], F32, name="h_last", bufs=PACK)
+            for u in range(PARTS):
                 nc.vector.scalar_tensor_tensor(
-                    out=h[:, u * BANK : (u + 1) * BANK],
-                    in0=resp[u][:],
+                    out=like(h[:, u * BANK : (u + 1) * BANK], cosine[u]),
+                    in0=like(resp[u][:], cosine[u]),
                     scalar=gain_t[:, b, t : t + 1],
-                    in1=cosine[u][:],
+                    in1=cosine[u],
                     op0=ALU.mult,
                     op1=ALU.mult,
                 )
             return h
 
         def pick_basal(planes, h, t, j0, width):
-            nc.vector.tensor_copy(out=planes[:, t, :], in_=h[:].indirect(pos2_t[:, j0 // 16 : (j0 + width) // 16]))
+            entries = pos2_t[:, j0 // PER_COLUMN : (j0 + width) // PER_COLUMN]
+            nc.vector.tensor_copy(out=planes[:, t, :], in_=h[:].indirect(entries))
 
         def pick_apical(planes, h, b, t, j0, width):
+            entries = pos1_t[:, j0 // PER_COLUMN : (j0 + width) // PER_COLUMN]
             nc.vector.tensor_tensor(
-                out=planes[:, t, :],
-                in0=h[:].indirect(pos1_t[:, j0 // 16 : (j0 + width) // 16]),
-                in1=prior_t[b][:, t, j0 : j0 + width],
-                op=ALU.add,
+                out=planes[:, t, :], in0=h[:].indirect(entries), in1=prior_t[b][:, t, j0 : j0 + width], op=ALU.add
             )
 
-        def round_basal(planes, width):
-            rounded = ring.tile([P, PACK * width], BF16, name="x_rounded", align_bytes=64, bufs=3)
+        def whole_rounded():
+            return ring.tile([P, PACK * J], BF16, name="x_rounded", align_bytes=64)[:]
+
+        def half_rounded():
+            return ring.tile([P, PACK * HALF], BF16, name="half_rounded", align_bytes=64, bufs=4)[:]
+
+        def round_basal(planes, rounded):
             dst, src = woven(rounded, planes)
             nc.scalar.activation(out=dst, in_=src, func=ACT.Abs)
             return rounded
 
-        def round_apical(planes, width):
-            rounded = ring.tile([P, PACK * width], BF16, name="x_rounded", align_bytes=64, bufs=3)
+        def round_apical(planes, rounded):
             dst, src = woven(rounded, planes)
             nc.scalar.copy(out=dst, in_=src)
             return rounded
 
-        def second_stage(banks, b, half, weight, x, x0):
-            for t in range(PACK):
-                lhsT, lhsT_scale = weight(b, t)
-                nc.tensor.matmul_mx(
-                    out=banks[half][t // 2][:, t % 2, :],
-                    lhsT=lhsT,
-                    lhsT_scale=lhsT_scale,
-                    rhs=x[0][:, x0 : x0 + HALF].bitcast(FP8X4),
-                    rhs_scale=x[1][:, x0 : x0 + HALF],
-                    start=(b == 0 and t % 2 == 0),
-                    stop=(b == BLOCKS - 1 and t % 2 == 1),
-                )
-
-        wb_q = {}
+        wb_q, xa_q, xb_q = {}, {}, {}
 
         def wb_slice(b, t):
             return wb_q[b][0][:, t * P : (t + 1) * P].bitcast(FP8X4), wb_q[b][1][:, t * P : (t + 1) * P]
 
         def w4_slice(b, t):
             c0 = b * N + t * P
-            return w4_codes[:, 2 * c0 : 2 * (c0 + P)].bitcast(FP4X4), w4_planes[:, c0 : c0 + P]
+            return w4_codes[:, 2 * c0 : 2 * (c0 + P)].bitcast(FP4X4), w4_dealt_scales[:, c0 : c0 + P]
 
-        yb_banks = [[psum.tile([P, 2, HALF], F32, name="yb") for pair in range(2)] for half in range(2)]
-        xa_q = {}
-        last = BLOCKS - 1
+        def second_stage(banks, b, weight, x, x0):
+            for t in range(PACK):
+                lhsT, lhsT_scale = weight(b, t)
+                nc.tensor.matmul_mx(
+                    out=banks[t // 2][:, t % 2, :],
+                    lhsT=lhsT,
+                    lhsT_scale=lhsT_scale,
+                    rhs=x[0][:, x0 : x0 + HALF].bitcast(FP8X4),
+                    rhs_scale=x[1][:, x0 : x0 + HALF],
+                    start=(b == 0 and t % 2 == 0),
+                    stop=(b == LAST and t % 2 == 1),
+                )
+
+        picked = {}
+
+        def next_w1(b):
+            w1_q[b] = quantize_weight(f"w1_{b}", w1_raw[b], b == 1)
+
+        def next_wb(b):
+            wb_q[b] = quantize_weight(f"wb_{b}", wb_raw[b], False)
+
+        def next_xb(b):
+            xb_q[b] = quantize(f"xb_{b}", round_basal(picked[b][:, 0, :, :], whole_rounded()), J)
+
+        def next_xa(b):
+            xa_q[b] = quantize(f"xa_{b}", round_apical(picked[b][:, 1, :, :], whole_rounded()), J)
+
+        rounding_after = {
+            1: [(next_w1, 1)],
+            PACK: [(next_wb, 0)],
+            PACK + 1: [(next_w1, 2)],
+            PACK + 2: [(next_xb, 0)],
+            PACK + 3: [(next_xa, 0)],
+            2 * PACK: [(next_wb, 1)],
+            3 * PACK - 1: [(next_xb, 1), (next_xa, 1), (next_wb, 2)],
+        }
+
         slices = [(b, t) for b in range(BLOCKS) for t in range(PACK)]
-        hs = {slices[0]: features(*slices[0])}
-        planes_a, planes_b = None, None
-        done = None
+        hs = {slices[0]: features(0, 0, [scratch("cosine") for u in range(PARTS)])}
         for s, (b, t) in enumerate(slices):
-            width = J if b < last else HALF
-            if t == 0:
-                planes_a = ring.tile([P, PACK, width], F32, name="planes_a")
-                planes_b = ring.tile([P, PACK, width], F32, name="planes_b")
-            if t == 1 and b < last:
-                w1_q[b + 1] = quantize(f"w1_{b + 1}", round_weight(w1_raw[b + 1], False), PASS)
-            if t == 2:
-                wb_q[b] = quantize(f"wb_{b}", round_weight(wb_raw[b], True), N)
+            width = J if b < LAST else HALF
+            if t == 0 and b < LAST:
+                picked[b] = ring.tile([P, 2, PACK, width], F32, name="picked")
+            elif t == 0:
+                picked[b] = keep.tile([P, 2, PACK, width], F32, name="picked_last")
             if s + 1 < len(slices):
-                hs[slices[s + 1]] = features(*slices[s + 1])
-            if t == 0 and done is not None:
-                xb_rounded = round_basal(done[1], J)
-                xa_rounded = round_apical(done[0], J)
-            pick_basal(planes_b, hs[b, t], t, 0, width)
-            pick_apical(planes_a, hs[b, t], b, t, 0, width)
-            if t == 0 and done is not None:
-                xb_q = quantize(f"xb_{b - 1}", xb_rounded, J)
-                xa_q[b - 1] = quantize(f"xa_{b - 1}", xa_rounded, J)
-                for half in range(2):
-                    second_stage(yb_banks, b - 1, half, wb_slice, xb_q, half * HALF)
-            if s == 0:
-                deal_w4()
-            if t == PACK - 1:
-                done = (planes_a, planes_b)
+                if s == 0:
+                    cosine = [scratch("cosine") for u in range(PARTS)]
+                elif b < LAST:
+                    cosine = [picked[b][:, 0, t, :], picked[b][:, 1, t, :]]
+                else:
+                    cosine = [picked[b][:, :, t, :], scratch("cosine")]
+                hs[slices[s + 1]] = features(*slices[s + 1], cosine)
+            for job, block in rounding_after.get(s + 1, []):
+                job(block)
+            pick_basal(picked[b][:, 0, :, :], hs[b, t], t, 0, width)
+            pick_apical(picked[b][:, 1, :, :], hs[b, t], b, t, 0, width)
 
-        ya_banks = [[psum.tile([P, 2, HALF], F32, name="resp") for pair in range(2)] for half in range(2)]
-        for b in range(last):
-            for half in range(2):
-                second_stage(ya_banks, b, half, w4_slice, xa_q[b], half * HALF)
+        yb_banks, ya_banks = {}, {}
+
+        def open_sums(half):
+            yb_banks[half] = [psum.tile([P, 2, HALF], F32, name="bank") for pair in range(2)]
+            for b in range(LAST):
+                second_stage(yb_banks[half], b, wb_slice, xb_q[b], half * HALF)
+            ya_banks[half] = [psum.tile([P, 2, HALF], F32, name="bank") for pair in range(2)]
+            for b in range(LAST):
+                second_stage(ya_banks[half], b, w4_slice, xa_q[b], half * HALF)
+
+        open_sums(0)
 
         y_codes = keep.tile([P, J], U32, name="y_codes", align_bytes=64)
         y_scales = keep.tile([P, J], U8, name="y_scales", align_bytes=64)
         out_rows = out_0.rearrange("(p t) j -> p t j", t=PACK)
         out_words = out_1[0].rearrange("p m t -> p (m t)").bitcast(I32)
 
-        def close_sums(half, xa_rounded, xb_rounded):
-            xb_q = quantize(f"xb_last{half}", xb_rounded, HALF)
-            second_stage(yb_banks, last, half, wb_slice, xb_q, 0)
-            xa_last = quantize(f"xa_last{half}", xa_rounded, HALF)
-            second_stage(ya_banks, last, half, w4_slice, xa_last, 0)
-
-        def product(half):
-            y = keep.tile([P, PACK, HALF], F32, name=f"y{half}")
+        def basal_sums_out(half):
+            sums = []
             for pair in range(2):
-                yb = ring.tile([P, 2, HALF], F32, name="yb_out")
+                yb = ring.tile([P, 2, HALF], F32, name="cosine", bufs=2 * PARTS)
                 nc.scalar.copy(out=yb[:], in_=yb_banks[half][pair][:])
-                nc.vector.tensor_tensor(out=y[:, 2 * pair : 2 * pair + 2, :], in0=ya_banks[half][pair][:], in1=yb[:], op=ALU.mult)
-            cols = slice(half * HALF, (half + 1) * HALF)
-            nc.sync.dma_start(out=out_rows[:, :, cols], in_=y[:])
-            rounded = ring.tile([P, PACK * HALF], BF16, name="w_rounded", align_bytes=64)
-            dst, src = woven(rounded, y)
-            nc.scalar.copy(out=dst, in_=src)
-            return rounded
+                sums.append(yb)
+            return sums
 
-        def planes_out(half, rounded):
+        def product(half, yb):
+            y = ring.tile([P, PACK, HALF], F32, name="h", bufs=3)
+            for pair in range(2):
+                nc.vector.tensor_tensor(
+                    out=y[:, 2 * pair : 2 * pair + 2, :], in0=ya_banks[half][pair][:], in1=yb[pair][:], op=ALU.mult
+                )
+            nc.sync.dma_start(out=out_rows[:, :, half * HALF : (half + 1) * HALF], in_=y[:])
+            return y
+
+        def codes_out(half, y, on_vector):
+            rounded = ring.tile([P, PACK * HALF], BF16, name="w_rounded", align_bytes=64)
+            copy_on(on_vector, *woven(rounded[:], y[:]))
             cols = slice(half * HALF, (half + 1) * HALF)
             nc.vector.quantize_mx(out=y_codes[:, cols].bitcast(FP8X4), scales=y_scales[:, cols], in_=rounded[:])
             nc.sync.dma_start(out=out_words[:, cols], in_=y_codes[:, cols].bitcast(I32))
 
-        xb_first = round_basal(done[1], HALF)
-        xa_first = round_apical(done[0], HALF)
-        planes_a = ring.tile([P, PACK, HALF], F32, name="planes_a")
-        planes_b = ring.tile([P, PACK, HALF], F32, name="planes_b")
+        second_a = picked[LAST][:].rearrange("p s t j -> p (s t) j")[:, PACK - 2 : PACK + 2, :]
+        second_b = picked[LAST - 1][:].rearrange("p s t (c j) -> p (s t c) j", c=2)[:, 2 * PACK - 2 : 2 * PACK + 2, :]
+        xb_first = round_basal(picked[LAST][:, 0, :, :], half_rounded())
+        xa_first = round_apical(picked[LAST][:, 1, :, :], half_rounded())
         for t in range(PACK):
-            pick_basal(planes_b, hs[last, t], t, HALF, HALF)
-        close_sums(0, xa_first, xb_first)
-        xb_second = round_basal(planes_b, HALF)
+            pick_basal(second_b, hs[LAST, t], t, HALF, HALF)
+        second_stage(yb_banks[0], LAST, wb_slice, quantize("xb_first", xb_first, HALF), 0)
+        second_stage(ya_banks[0], LAST, w4_slice, quantize("xa_first", xa_first, HALF), 0)
+        open_sums(1)
+        xb_second = round_basal(second_b, half_rounded())
+        yb_first = basal_sums_out(0)
         for t in range(PACK):
-            pick_apical(planes_a, hs[last, t], last, t, HALF, HALF)
-        xa_second = round_apical(planes_a, HALF)
-        y_first = product(0)
-        close_sums(1, xa_second, xb_second)
-        planes_out(0, y_first)
-        planes_out(1, product(1))
-        for q in range(4):
-            nc.sync.dma_start(
-                out=out_2[0, 4 * q : 4 * q + 4, :].bitcast(I32), in_=y_scales[32 * q : 32 * q + 4, :].bitcast(I32)
+            pick_apical(second_a, hs[LAST, t], LAST, t, HALF, HALF)
+        second_stage(yb_banks[1], LAST, wb_slice, quantize("xb_second", xb_second, HALF), 0)
+        xa_second = round_apical(second_a, half_rounded())
+        yb_second = basal_sums_out(1)
+        y_first = product(0, yb_first)
+        second_stage(ya_banks[1], LAST, w4_slice, quantize("xa_second", xa_second, HALF), 0)
+        codes_out(0, y_first, False)
+        codes_out(1, product(1, yb_second), True)
+        for r in range(PACK):
+            (nc.sync if r % 2 else nc.scalar).dma_start(
+                out=out_2[0, r:SCALE_ROWS:PACK, :].bitcast(I32), in_=y_scales[r:P:QUADRANT, :].bitcast(I32)
             )

import math
from contextlib import ExitStack

import concourse.mybir as mybir

K, T, S, J, H, N = 512, 4096, 1024, 512, 1536, 512
FLOPS = 2 * K * H * S + 2 * 2 * H * N * J

F32 = mybir.dt.float32
BF16 = mybir.dt.bfloat16
I32 = mybir.dt.int32
U32 = mybir.dt.uint32
U16 = mybir.dt.uint16
U8 = mybir.dt.uint8
FP8X4 = mybir.dt.float8_e4m3fn_x4
FP4X4 = mybir.dt.float4_e2m1fn_x4
ACT = mybir.ActivationFunctionType
ALU = mybir.AluOpType

P = 128
PACK = 4
PASS = P * PACK
BLOCKS = H // PASS
LAST = BLOCKS - 1
BANK = 512
PARTS = S // BANK
HALF = J // 2
PER_COLUMN = 16
QUADRANT = 32
SCALE_ROWS = 16
RUN = 4


def tile_list_electrode_mapping_features_kernel(
    tc, tab_words, tab_scales, offs, pos1, pos2, w1, phase, gain, prior, w4_words, w4_scales, wb, out_0, out_1, out_2
):
    nc = tc.nc
    with ExitStack() as ctx:
        lists = ctx.enter_context(tc.tile_pool(name="lists", bufs=1))
        keep = ctx.enter_context(tc.tile_pool(name="keep", bufs=1))
        ring = ctx.enter_context(tc.tile_pool(name="ring", bufs=2))
        psum = ctx.enter_context(tc.psum_pool(name="psum", bufs=8))

        offs_t = lists.tile([P, S // PER_COLUMN], U16, name="offs_t")
        pos1_t = lists.tile([P, J // PER_COLUMN], U16, name="pos1_t")
        pos2_t = lists.tile([P, J // PER_COLUMN], U16, name="pos2_t")
        table_words = keep.tile([P, T], U32, name="table_words", align_bytes=64)
        table_scales = keep.tile([P, T], U8, name="table_scales", align_bytes=64)
        w4_raw = keep.tile([P, BLOCKS * N * 2], U8, name="w4_raw", align_bytes=64)
        w4_raw_scales = keep.tile([P, BLOCKS, N], U8, name="w4_raw_scales", align_bytes=64)
        phase_t = keep.tile([P, BLOCKS, PACK], F32, name="phase_t")
        gain_t = keep.tile([P, BLOCKS, PACK], F32, name="gain_t")
        w1_raw = [keep.tile([P, PACK, PASS], F32, name=f"w1_raw{b}") for b in range(BLOCKS)]
        wb_raw = [ring.tile([P, PACK, N], F32, name="wb_raw") for b in range(BLOCKS)]
        prior_t = [ring.tile([P, PACK, J], F32, name="prior_t") for b in range(BLOCKS)]

        def load_w1(b):
            nc.sync.dma_start(out=w1_raw[b][:], in_=w1[:, b * PASS : (b + 1) * PASS].rearrange("(p i) c -> p i c", i=PACK))

        def load_rows(dst, src, b):
            nc.sync.dma_start(out=dst[b][:], in_=src[b * PASS : (b + 1) * PASS, :].rearrange("(p i) c -> p i c", i=PACK))

        def load_per_row(dst, src):
            nc.sync.dma_start(out=dst[:], in_=src.rearrange("(b p t) -> p b t", p=P, t=PACK))

        warm = keep.tile([P, 1], F32, name="warm")
        warm_out = keep.tile([P, 1], F32, name="warm_out")
        nc.vector.memset(table_scales[:].bitcast(I32), 0)
        nc.gpsimd.memset(w4_raw_scales[:].rearrange("p a n -> p (a n)").bitcast(I32), 0)

        nc.sync.dma_start(offs_t[:], offs)
        load_w1(0)
        for r in range(PACK):
            nc.sync.dma_start(
                out=table_scales[r:P:QUADRANT, :].bitcast(I32), in_=tab_scales[0, r:SCALE_ROWS:PACK, :].bitcast(I32)
            )
        nc.gpsimd.memset(warm[:], 0.0)
        nc.scalar.activation(out=warm_out[:], in_=warm[:], func=ACT.Sin)
        nc.sync.dma_start(out=table_words[:].bitcast(I32), in_=tab_words[0].rearrange("p t i -> p (t i)").bitcast(I32))
        nc.sync.dma_start(
            out=w4_raw[:].bitcast(I32).rearrange("p (a c) -> p a c", a=BLOCKS),
            in_=w4_words.bitcast(I32).rearrange("a p c -> p a c"),
        )
        load_per_row(phase_t, phase)
        load_w1(1)
        for r in range(PACK):
            nc.sync.dma_start(
                out=w4_raw_scales[r:P:QUADRANT, :, :].bitcast(I32),
                in_=w4_scales[:, r:SCALE_ROWS:PACK, :].bitcast(I32).rearrange("a q c -> q a c"),
            )
        load_per_row(gain_t, gain)
        nc.sync.dma_start(pos2_t[:], pos2)
        nc.sync.dma_start(pos1_t[:], pos1)
        load_rows(prior_t, prior, 0)
        load_rows(wb_raw, wb, 0)
        load_rows(prior_t, prior, 1)
        load_w1(2)
        load_rows(wb_raw, wb, 1)
        load_rows(prior_t, prior, 2)
        load_rows(wb_raw, wb, 2)

        def quantize(name, rounded, width):
            codes = keep.tile([P, width], U32, name=name + "_codes", align_bytes=64)
            scales = keep.tile([P, width], U8, name=name + "_scales", align_bytes=64)
            nc.vector.quantize_mx(out=codes[:].bitcast(FP8X4), scales=scales[:], in_=rounded)
            return codes, scales

        def copy_on(on_vector, dst, src):
            if on_vector:
                nc.vector.tensor_copy(out=dst, in_=src)
            else:
                nc.scalar.copy(out=dst, in_=src)

        def quantize_weight(name, raw, on_vector):
            rounded = ring.tile([P, PACK * PASS], BF16, name="w_rounded", align_bytes=64)
            copy_on(
                on_vector,
                rounded[:].rearrange("p (t m i) -> p m i t", t=PACK, i=PACK),
                raw[:].rearrange("p i (m t) -> p m i t", t=PACK),
            )
            return quantize(name, rounded[:], PASS)

        def woven(rounded, planes):
            return (
                rounded.rearrange("p (c i t) -> p c t i", i=RUN, t=PACK),
                planes.rearrange("p t (c i) -> p c t i", i=RUN),
            )

        v_scales = keep.tile([P, S], U8, name="v_scales", align_bytes=64)
        nc.vector.tensor_copy(out=v_scales[:], in_=table_scales[:].indirect(offs_t[:]))
        w1_q = {0: quantize_weight("w1_0", w1_raw[0], True)}
        w4_codes = keep.tile([P, BLOCKS * N * 2], U8, name="w4_codes", align_bytes=64)
        w4_dealt_scales = keep.tile([P, BLOCKS * N], U8, name="w4_dealt_scales", align_bytes=64)
        v_words = []
        for u in range(PARTS):
            words = keep.tile([P, BANK], U32, name=f"v_words{u}", align_bytes=64)
            entries = offs_t[:, u * BANK // PER_COLUMN : (u + 1) * BANK // PER_COLUMN]
            nc.vector.tensor_copy(out=words[:], in_=table_words[:].indirect(entries))
            v_words.append(words)

        nc.vector.tensor_copy(
            out=w4_codes[:].bitcast(U16).rearrange("p (a t m) -> p a t m", a=BLOCKS, t=PACK),
            in_=w4_raw[:].bitcast(U16).rearrange("p (a m t) -> p a t m", a=BLOCKS, t=PACK),
        )
        nc.vector.tensor_copy(
            out=w4_dealt_scales[:].rearrange("p (a t m) -> p a t m", a=BLOCKS, t=PACK),
            in_=w4_raw_scales[:].rearrange("p a (m t) -> p a t m", t=PACK),
        )

        def like(flat, other):
            return flat if len(other.shape) == 2 else flat.rearrange("p (r j) -> p r j", r=other.shape[1])

        def scratch(name):
            return ring.tile([P, BANK], F32, name=name, bufs=2 * PARTS)[:]

        def features(b, t, cosine):
            folded = [scratch("folded") for u in range(PARTS)]
            codes, scales = w1_q[b]
            cols = slice(t * P, (t + 1) * P)
            resp = []
            for u in range(PARTS):
                bank = psum.tile([P, BANK], F32, name="bank")
                nc.tensor.matmul_mx(
                    out=bank[:],
                    lhsT=codes[:, cols].bitcast(FP8X4),
                    lhsT_scale=scales[:, cols],
                    rhs=v_words[u][:].bitcast(FP8X4),
                    rhs_scale=v_scales[:, u * BANK : (u + 1) * BANK],
                    start=True,
                    stop=True,
                )
                resp.append(bank)
            for u in range(PARTS):
                nc.scalar.activation(out=folded[u], in_=resp[u][:], func=ACT.Abs, bias=phase_t[:, b, t : t + 1])
            for u in range(PARTS):
                nc.scalar.activation(out=cosine[u], in_=like(folded[u], cosine[u]), func=ACT.Sin, scale=-1.0, bias=math.pi / 2)
            if b < LAST:
                h = ring.tile([P, S], F32, name="h", bufs=3)
            else:
                h = ring.tile([P, S], F32, name="h_last", bufs=PACK)
            for u in range(PARTS):
                nc.vector.scalar_tensor_tensor(
                    out=like(h[:, u * BANK : (u + 1) * BANK], cosine[u]),
                    in0=like(resp[u][:], cosine[u]),
                    scalar=gain_t[:, b, t : t + 1],
                    in1=cosine[u],
                    op0=ALU.mult,
                    op1=ALU.mult,
                )
            return h

        def pick_basal(planes, h, t, j0, width):
            entries = pos2_t[:, j0 // PER_COLUMN : (j0 + width) // PER_COLUMN]
            nc.vector.tensor_copy(out=planes[:, t, :], in_=h[:].indirect(entries))

        def pick_apical(planes, h, b, t, j0, width):
            entries = pos1_t[:, j0 // PER_COLUMN : (j0 + width) // PER_COLUMN]
            nc.vector.tensor_tensor(
                out=planes[:, t, :], in0=h[:].indirect(entries), in1=prior_t[b][:, t, j0 : j0 + width], op=ALU.add
            )

        def whole_rounded():
            return ring.tile([P, PACK * J], BF16, name="x_rounded", align_bytes=64)[:]

        def half_rounded():
            return ring.tile([P, PACK * HALF], BF16, name="half_rounded", align_bytes=64, bufs=4)[:]

        def round_basal(planes, rounded):
            dst, src = woven(rounded, planes)
            nc.scalar.activation(out=dst, in_=src, func=ACT.Abs)
            return rounded

        def round_apical(planes, rounded):
            dst, src = woven(rounded, planes)
            nc.scalar.copy(out=dst, in_=src)
            return rounded

        wb_q, xa_q, xb_q = {}, {}, {}

        def wb_slice(b, t):
            return wb_q[b][0][:, t * P : (t + 1) * P].bitcast(FP8X4), wb_q[b][1][:, t * P : (t + 1) * P]

        def w4_slice(b, t):
            c0 = b * N + t * P
            return w4_codes[:, 2 * c0 : 2 * (c0 + P)].bitcast(FP4X4), w4_dealt_scales[:, c0 : c0 + P]

        def second_stage(banks, b, weight, x, x0):
            for t in range(PACK):
                lhsT, lhsT_scale = weight(b, t)
                nc.tensor.matmul_mx(
                    out=banks[t // 2][:, t % 2, :],
                    lhsT=lhsT,
                    lhsT_scale=lhsT_scale,
                    rhs=x[0][:, x0 : x0 + HALF].bitcast(FP8X4),
                    rhs_scale=x[1][:, x0 : x0 + HALF],
                    start=(b == 0 and t % 2 == 0),
                    stop=(b == LAST and t % 2 == 1),
                )

        picked = {}

        def next_w1(b):
            w1_q[b] = quantize_weight(f"w1_{b}", w1_raw[b], b == 1)

        def next_wb(b):
            wb_q[b] = quantize_weight(f"wb_{b}", wb_raw[b], False)

        def next_xb(b):
            xb_q[b] = quantize(f"xb_{b}", round_basal(picked[b][:, 0, :, :], whole_rounded()), J)

        def next_xa(b):
            xa_q[b] = quantize(f"xa_{b}", round_apical(picked[b][:, 1, :, :], whole_rounded()), J)

        rounding_after = {
            1: [(next_w1, 1)],
            PACK: [(next_wb, 0)],
            PACK + 1: [(next_w1, 2)],
            PACK + 2: [(next_xb, 0)],
            PACK + 3: [(next_xa, 0)],
            2 * PACK: [(next_wb, 1)],
            3 * PACK - 1: [(next_xb, 1), (next_xa, 1), (next_wb, 2)],
        }

        slices = [(b, t) for b in range(BLOCKS) for t in range(PACK)]
        hs = {slices[0]: features(0, 0, [scratch("cosine") for u in range(PARTS)])}
        for s, (b, t) in enumerate(slices):
            width = J if b < LAST else HALF
            if t == 0 and b < LAST:
                picked[b] = ring.tile([P, 2, PACK, width], F32, name="picked")
            elif t == 0:
                picked[b] = keep.tile([P, 2, PACK, width], F32, name="picked_last")
            if s + 1 < len(slices):
                if s == 0:
                    cosine = [scratch("cosine") for u in range(PARTS)]
                elif b < LAST:
                    cosine = [picked[b][:, 0, t, :], picked[b][:, 1, t, :]]
                else:
                    cosine = [picked[b][:, :, t, :], scratch("cosine")]
                hs[slices[s + 1]] = features(*slices[s + 1], cosine)
            for job, block in rounding_after.get(s + 1, []):
                job(block)
            pick_basal(picked[b][:, 0, :, :], hs[b, t], t, 0, width)
            pick_apical(picked[b][:, 1, :, :], hs[b, t], b, t, 0, width)

        yb_banks, ya_banks = {}, {}

        def open_sums(half):
            yb_banks[half] = [psum.tile([P, 2, HALF], F32, name="bank") for pair in range(2)]
            for b in range(LAST):
                second_stage(yb_banks[half], b, wb_slice, xb_q[b], half * HALF)
            ya_banks[half] = [psum.tile([P, 2, HALF], F32, name="bank") for pair in range(2)]
            for b in range(LAST):
                second_stage(ya_banks[half], b, w4_slice, xa_q[b], half * HALF)

        open_sums(0)

        y_codes = keep.tile([P, J], U32, name="y_codes", align_bytes=64)
        y_scales = keep.tile([P, J], U8, name="y_scales", align_bytes=64)
        out_rows = out_0.rearrange("(p t) j -> p t j", t=PACK)
        out_words = out_1[0].rearrange("p m t -> p (m t)").bitcast(I32)

        def basal_sums_out(half):
            sums = []
            for pair in range(2):
                yb = ring.tile([P, 2, HALF], F32, name="cosine", bufs=2 * PARTS)
                nc.scalar.copy(out=yb[:], in_=yb_banks[half][pair][:])
                sums.append(yb)
            return sums

        def product(half, yb):
            y = ring.tile([P, PACK, HALF], F32, name="h", bufs=3)
            for pair in range(2):
                nc.vector.tensor_tensor(
                    out=y[:, 2 * pair : 2 * pair + 2, :], in0=ya_banks[half][pair][:], in1=yb[pair][:], op=ALU.mult
                )
            nc.sync.dma_start(out=out_rows[:, :, half * HALF : (half + 1) * HALF], in_=y[:])
            return y

        def codes_out(half, y, on_vector):
            rounded = ring.tile([P, PACK * HALF], BF16, name="w_rounded", align_bytes=64)
            copy_on(on_vector, *woven(rounded[:], y[:]))
            cols = slice(half * HALF, (half + 1) * HALF)
            nc.vector.quantize_mx(out=y_codes[:, cols].bitcast(FP8X4), scales=y_scales[:, cols], in_=rounded[:])
            nc.sync.dma_start(out=out_words[:, cols], in_=y_codes[:, cols].bitcast(I32))

        second_a = picked[LAST][:].rearrange("p s t j -> p (s t) j")[:, PACK - 2 : PACK + 2, :]
        second_b = picked[LAST - 1][:].rearrange("p s t (c j) -> p (s t c) j", c=2)[:, 2 * PACK - 2 : 2 * PACK + 2, :]
        xb_first = round_basal(picked[LAST][:, 0, :, :], half_rounded())
        xa_first = round_apical(picked[LAST][:, 1, :, :], half_rounded())
        for t in range(PACK):
            pick_basal(second_b, hs[LAST, t], t, HALF, HALF)
        second_stage(yb_banks[0], LAST, wb_slice, quantize("xb_first", xb_first, HALF), 0)
        second_stage(ya_banks[0], LAST, w4_slice, quantize("xa_first", xa_first, HALF), 0)
        open_sums(1)
        xb_second = round_basal(second_b, half_rounded())
        yb_first = basal_sums_out(0)
        for t in range(PACK):
            pick_apical(second_a, hs[LAST, t], LAST, t, HALF, HALF)
        second_stage(yb_banks[1], LAST, wb_slice, quantize("xb_second", xb_second, HALF), 0)
        xa_second = round_apical(second_a, half_rounded())
        yb_second = basal_sums_out(1)
        y_first = product(0, yb_first)
        second_stage(ya_banks[1], LAST, w4_slice, quantize("xa_second", xa_second, HALF), 0)
        codes_out(0, y_first, False)
        codes_out(1, product(1, yb_second), True)
        for r in range(PACK):
            (nc.sync if r % 2 else nc.scalar).dma_start(
                out=out_2[0, r:SCALE_ROWS:PACK, :].bitcast(I32), in_=y_scales[r:P:QUADRANT, :].bitcast(I32)
            )
